import numpy as np
import ml_dtypes


def mxq(x, axis, fmt="e4m3"):
    dtype, down = {"e4m3": (ml_dtypes.float8_e4m3fn, 7), "e5m2": (ml_dtypes.float8_e5m2, 14)}[fmt]
    v = np.moveaxis(np.asarray(x, np.float32).astype(ml_dtypes.bfloat16).astype(np.float64), axis, -1)
    blocks = v.reshape(v.shape[:-1] + (-1, 32))
    amax = np.abs(blocks).max(-1, keepdims=True)
    byte = np.maximum(np.where(amax > 0, np.frexp(amax)[1] - 1 + 127, 0) - down, 1)
    scale = np.exp2(byte - 127.0)
    codes = (blocks / scale).astype(np.float32).astype(dtype).astype(np.float64)
    return np.moveaxis((codes * scale).reshape(v.shape), -1, axis)


WIDE = False


def mx_kscale(k):
    if not WIDE:
        return np.ones(k)
    levels = np.array([30, -30])
    if k % 512:
        return np.exp2(np.random.permutation(np.resize(levels, k // 32))).repeat(32)
    a = np.empty((k // 512, 16))
    for p in range(k // 512):
        a[p, :8] = np.random.permutation(np.resize(levels, 8))
        for g in range(8):
            far = levels[np.abs(levels - a[p, g]) >= 10]
            a[p, g + 8] = far[np.random.randint(len(far))]
    return np.exp2(a.ravel()).repeat(32)


def f64(x):
    return np.asarray(x).astype(np.float64)


def striped(idx):
    return np.tile(np.asarray(idx).reshape(-1, 16).T, (8, 1)).astype(np.uint16)


def unstriped(offs):
    return offs[:16].T.reshape(-1).astype(np.int64)


E2M1 = np.array([0.0, 0.5, 1.0, 1.5, 2.0, 3.0, 4.0, 6.0, -0.0, -0.5, -1.0, -1.5, -2.0, -3.0, -4.0, -6.0])


def pack_weight(w, fmt):
    k, n = w.shape
    w = f64(np.asarray(w, np.float32).astype(ml_dtypes.bfloat16)).reshape(k // 32, 32, n)
    amax = np.abs(w).max(1)
    if fmt in ("e4m3", "e5m2"):
        byte = np.frexp(amax)[1] - 1 + 127 - (7 if fmt == "e4m3" else 14)
    else:
        mant, ex = np.frexp(amax / 6.0)
        byte = np.where(mant > 0.5, ex, ex - 1) + 127
    byte = np.clip(np.where(amax > 0, byte, 1), 1, 254)
    scaled = (w * np.exp2(127.0 - byte)[:, None, :]).reshape(k, n).astype(np.float32)
    by_word = np.ascontiguousarray(scaled.reshape(k // 512, 128, 4, n).transpose(0, 1, 3, 2))
    if fmt in ("e4m3", "e5m2"):
        words = by_word.astype(ml_dtypes.float8_e4m3fn if fmt == "e4m3" else ml_dtypes.float8_e5m2).view(np.uint8)
    else:
        c = by_word.astype(ml_dtypes.float4_e2m1fn).view(np.uint8) & 0xF
        words = (c[..., 0::2] | (c[..., 1::2] << 4)).reshape(k // 512, 128, 2 * n)
    return np.ascontiguousarray(words), np.ascontiguousarray(byte.astype(np.uint8).reshape(k // 512, 16, n))


def unpack_weight(words, scales, fmt):
    g, _, n = scales.shape
    words = np.ascontiguousarray(words).reshape(g, 128, n, -1)
    if fmt in ("e4m3", "e5m2"):
        vals = words.view(ml_dtypes.float8_e4m3fn if fmt == "e4m3" else ml_dtypes.float8_e5m2).astype(np.float64)
    else:
        nib = np.empty((g, 128, n, 4), np.uint8)
        nib[..., 0::2] = words & 0xF
        nib[..., 1::2] = words >> 4
        vals = E2M1[nib]
    vals = vals * np.repeat(np.exp2(scales.astype(np.float64) - 127.0), 8, axis=1)[..., None]
    return vals.transpose(0, 1, 3, 2).reshape(g * 512, n)


def e4m3fn_bytes(y):
    return np.clip(np.asarray(y, np.float64), -448.0, 448.0).astype(np.float32).astype(ml_dtypes.float8_e4m3fn).view(np.uint8)


def e4m3fn_values(b):
    return np.asarray(b, np.uint8).view(ml_dtypes.float8_e4m3fn).astype(np.float64)


K, T, J, R, F, Z, V, N, E = 512, 1024, 256, 512, 512, 1024, 1024, 256, 1024


def setup_inputs():
    n = np.random.standard_normal
    idx = np.random.permutation(T)[:J]
    idx2 = np.random.permutation(Z)[:J]
    idx3 = np.random.permutation(V)[:J]
    idx4 = np.random.permutation(E)[:J]
    fk = mx_kscale(K)
    ff = mx_kscale(F)
    fr = mx_kscale(R)
    xtp = pack_weight(n((K, T)) / fk[:, None], "e4m3")
    xop = pack_weight(n((F, Z)) / ff[:, None], "e2m1")
    wp = pack_weight(n((K, R)) * 1 / np.sqrt(K) * fk[:, None] * fr, "e2m1")
    w2p = pack_weight(n((F, R)) * 1 / np.sqrt(F) * ff[:, None] * fr, "e5m2")
    wbp = pack_weight(n((R, N)) * 1 / np.sqrt(R) / fr[:, None], "e5m2")
    return {
        "xt_words": xtp[0],
        "xt_scales": xtp[1],
        "xo_words": xop[0],
        "xo_scales": xop[1],
        "w_words": wp[0],
        "w_scales": wp[1],
        "w2_words": w2p[0],
        "w2_scales": w2p[1],
        "ca": e4m3fn_bytes(60.0 * n((R, V))),
        "st": (np.random.uniform(0.008, 0.024, (R, 1)) * fr[:, None]).astype(np.float32),
        "wb_words": wbp[0],
        "wb_scales": wbp[1],
        "so": (np.random.uniform(0.5, 1.6, (N, 1))).astype(np.float32),
        "offs": striped(idx),
        "offs2": striped(idx2),
        "offs3": striped(idx3),
        "offs4": striped(idx4),
    }


def reference(xt_words, xt_scales, xo_words, xo_scales, w_words, w_scales, w2_words, w2_scales, ca, st, wb_words, wb_scales, so, offs, offs2, offs3, offs4):
    idx = unstriped(offs)
    idx2 = unstriped(offs2)
    idx3 = unstriped(offs3)
    idx4 = unstriped(offs4)
    xtu = unpack_weight(xt_words, xt_scales, "e4m3")
    xou = unpack_weight(xo_words, xo_scales, "e2m1")
    wu = unpack_weight(w_words, w_scales, "e2m1")
    w2u = unpack_weight(w2_words, w2_scales, "e5m2")
    wbu = unpack_weight(wb_words, wb_scales, "e5m2")
    xtidxg = xtu[:, idx]
    a = wu.T @ xtidxg
    xoidx2g = xou[:, idx2]
    b = w2u.T @ xoidx2g
    g1 = e4m3fn_values(ca)[:, idx3] * f64(st)
    hid = np.minimum(np.abs(a - g1), np.abs(b - g1))
    hidq = mxq(hid, 0, "e4m3")
    p = wbu.T @ hidq
    y = np.zeros((N, E))
    y[:, idx4] = p * f64(so)
    return y

@@ -1,0 +1,193 @@
+from contextlib import ExitStack
+
+import concourse.mybir as mybir
+
+K, T, J, R, N, E = 512, 1024, 256, 512, 256, 1024
+FLOPS = 2 * K * R * J * 2 + 2 * R * N * J
+
+F32 = mybir.dt.float32
+BF16 = mybir.dt.bfloat16
+I32 = mybir.dt.int32
+U32 = mybir.dt.uint32
+U16 = mybir.dt.uint16
+U8 = mybir.dt.uint8
+FP8 = mybir.dt.float8_e4m3fn
+E4M3 = mybir.dt.float8_e4m3fn_x4
+E5M2 = mybir.dt.float8_e5m2_x4
+E2M1 = mybir.dt.float4_e2m1fn_x4
+ACT = mybir.ActivationFunctionType
+ALU = mybir.AluOpType
+
+P = 128
+PACK = 4
+HALVES = 2
+JH = J // HALVES
+LIST_COLS = J // 16
+
+
+def tile_list_nearerresult_kernel(tc, xt_words, xt_scales, xo_words, xo_scales, w_words, w_scales,
+                                       w2_words, w2_scales, ca, st, wb_words, wb_scales, so,
+                                       offs, offs2, offs3, offs4, out):
+    nc = tc.nc
+    with ExitStack() as ctx:
+        sb = ctx.enter_context(tc.tile_pool(name="sb", bufs=1))
+        ps = ctx.enter_context(tc.psum_pool(name="ps", bufs=1))
+
+        def tile(shape, dtype, name):
+            return sb.tile(shape, dtype, name=name, align_bytes=64)
+
+        lists = [tile([P, LIST_COLS], U16, "list%d" % i) for i in range(4)]
+        xt_list, xo_list, ca_list, page_list = lists
+
+        xt_w = tile([P, T], U32, "xt_w")
+        xt_s = tile([P, T], U8, "xt_s")
+        xo_w = tile([P, T], U16, "xo_w")
+        xo_s = tile([P, T], U8, "xo_s")
+        w_w = tile([P, R], U16, "w_w")
+        w_s = tile([P, 2, R], U8, "w_s")
+        w2_w = tile([P, R], U32, "w2_w")
+        w2_s = tile([P, 2, R], U8, "w2_s")
+        wb_w = tile([P, N], U32, "wb_w")
+        wb_s = tile([P, N], U8, "wb_s")
+        ca_rows = [tile([P, T], U8, "ca_rows%d" % t) for t in range(PACK)]
+        st_sb = tile([P, PACK], F32, "st_sb")
+        so_sb = tile([P, N // P], F32, "so_sb")
+        pages = [tile([P, E], F32, "page%d" % c) for c in range(N // P)]
+
+        nc.vector.memset(xt_s[:].bitcast(I32), 0)
+        nc.vector.memset(w_s[:].rearrange("p h c -> p (h c)").bitcast(I32), 0)
+        nc.vector.memset(xo_s[:].bitcast(I32), 0)
+        nc.vector.memset(w2_s[:].rearrange("p h c -> p (h c)").bitcast(I32), 0)
+        nc.vector.memset(wb_s[:].bitcast(I32), 0)
+        for page in pages:
+            nc.vector.memset(page[:].bitcast(I32), 0)
+
+        ca_by_slot = ca.rearrange("(p t) v -> p t v", t=PACK)
+
+        def load_scale_rows(queue, plane, scales):
+            rows = scales[0].bitcast(I32)
+            for q in range(4):
+                queue.dma_start(plane[32 * q : 32 * q + 4, :].bitcast(I32), rows[4 * q : 4 * q + 4, :])
+
+        def load_scale_rows_paired(plane, scales):
+            rows = scales[0].bitcast(I32).rearrange("(h q r) c -> q r h c", h=2, q=2)
+            for q in range(2):
+                nc.sync.dma_start(plane[32 * q : 32 * q + 4, :, :].bitcast(I32), rows[q])
+
+        nc.sync.dma_start(ca_list[:], offs3)
+        nc.sync.dma_start(ca_rows[0][:], ca_by_slot[:, 0, :])
+        nc.sync.dma_start(xt_list[:], offs)
+        nc.scalar.dma_start(xt_w[:].bitcast(I32), xt_words[0].rearrange("p c r -> p (c r)").bitcast(I32))
+        load_scale_rows(nc.scalar, xt_s, xt_scales)
+        nc.sync.dma_start(ca_rows[1][:], ca_by_slot[:, 1, :])
+        load_scale_rows_paired(w_s, w_scales)
+        nc.sync.dma_start(w_w[:].bitcast(I32), w_words[0].bitcast(I32))
+        nc.sync.dma_start(ca_rows[2][:], ca_by_slot[:, 2, :])
+        nc.sync.dma_start(xo_list[:], offs2)
+        nc.sync.dma_start(xo_w[:].bitcast(I32), xo_words[0].bitcast(I32))
+        nc.sync.dma_start(w2_w[:].bitcast(I32), w2_words[0].rearrange("p c r -> p (c r)").bitcast(I32))
+        load_scale_rows(nc.sync, xo_s, xo_scales)
+        load_scale_rows_paired(w2_s, w2_scales)
+        nc.sync.dma_start(ca_rows[3][:], ca_by_slot[:, 3, :])
+        nc.sync.dma_start(page_list[:], offs4)
+        nc.gpsimd.dma_start(st_sb[:], st.rearrange("(p t) o -> p (t o)", t=PACK))
+        nc.gpsimd.dma_start(wb_w[:].bitcast(I32), wb_words[0].rearrange("p c r -> p (c r)").bitcast(I32))
+        load_scale_rows(nc.gpsimd, wb_s, wb_scales)
+        with nc.allow_non_contiguous_dma(reason="one weight a partition for each of the two row tiles"):
+            nc.gpsimd.dma_start(so_sb[:], so.rearrange("(c p) o -> p (c o)", p=P))
+
+        ca_g = [tile([P, J], U8, "ca_g%d" % t) for t in range(PACK)]
+        proto = tile([P, PACK, J], F32, "proto")
+        xt_gw = tile([P, J], U32, "xt_gw")
+        xt_gs = tile([P, J], U8, "xt_gs")
+        xo_gw = tile([P, J], U16, "xo_gw")
+        xo_gs = tile([P, J], U8, "xo_gs")
+        w_dw = tile([P, R], U16, "w_dw")
+        w_ds = tile([P, R], U8, "w_ds")
+        w2_dw = tile([P, R], U32, "w2_dw")
+        w2_ds = tile([P, R], U8, "w2_ds")
+
+        def look_up_prototypes(t):
+            nc.vector.tensor_copy(ca_g[t][:], ca_rows[t][:].indirect(ca_list[:]))
+            nc.scalar.activation(out=proto[:, t, :], in_=ca_g[t][:].bitcast(FP8), func=ACT.Copy, scale=st_sb[:, t : t + 1])
+
+        def deal_views(dst, src, run):
+            return (dst.rearrange("p (t c i) -> p c t i", t=PACK, i=run),
+                    src.rearrange("p (c i t) -> p c t i", t=PACK, i=run))
+
+        def deal_scales(dst, plane):
+            nc.vector.tensor_copy(plane[64:128, 0, :].bitcast(I32), plane[0:64, 1, :].bitcast(I32))
+            o, i = deal_views(dst[:], plane[:, 0, :], 16)
+            nc.vector.tensor_copy(o, i)
+
+        look_up_prototypes(0)
+        nc.vector.tensor_copy(xt_gw[:], xt_w[:].indirect(xt_list[:]))
+        nc.vector.tensor_copy(xt_gs[:], xt_s[:].indirect(xt_list[:]))
+        look_up_prototypes(1)
+        o, i = deal_views(w_dw[:], w_w[:], 8)
+        nc.scalar.copy(o, i)
+        deal_scales(w_ds, w_s)
+        look_up_prototypes(2)
+        nc.vector.tensor_copy(xo_gw[:], xo_w[:].indirect(xo_list[:]))
+        nc.vector.tensor_copy(xo_gs[:], xo_s[:].indirect(xo_list[:]))
+        o, i = deal_views(w2_dw[:], w2_w[:], 4)
+        nc.scalar.copy(o, i)
+        look_up_prototypes(3)
+        deal_scales(w2_ds, w2_s)
+
+        def first_stage(name, h, words, scales, wfmt, gwords, gscales, xfmt):
+            acc = ps.tile([P, PACK, JH], F32, name="%s%d" % (name, h))
+            cols = slice(h * JH, (h + 1) * JH)
+            for t in range(PACK):
+                rows = slice(t * P, (t + 1) * P)
+                nc.tensor.matmul_mx(out=acc[:, t, :], lhsT=words[:, rows].bitcast(wfmt), lhsT_scale=scales[:, rows],
+                                    rhs=gwords[:, cols].bitcast(xfmt), rhs_scale=gscales[:, cols], start=True, stop=True)
+            return acc
+
+        acc_a = [first_stage("acc_a", h, w_dw, w_ds, E2M1, xt_gw, xt_gs, E4M3) for h in range(HALVES)]
+        acc_b = [first_stage("acc_b", h, w2_dw, w2_ds, E5M2, xo_gw, xo_gs, E2M1) for h in range(HALVES)]
+
+        def distance(name, h, acc):
+            diff = tile([P, PACK, JH], F32, "diff_%s%d" % (name, h))
+            dist = tile([P, JH, PACK], F32, "dist_%s%d" % (name, h))
+            nc.vector.tensor_tensor(diff[:], acc[:], proto[:, :, h * JH : (h + 1) * JH], ALU.subtract)
+            nc.scalar.activation(out=dist[:], in_=diff[:].rearrange("p t j -> p j t"), func=ACT.Abs)
+            return dist
+
+        def nearer(h, dist_a, dist_b):
+            hid = tile([P, JH * PACK], BF16, "hid%d" % h)
+            nc.vector.tensor_tensor(hid[:], dist_a[:].rearrange("p j t -> p (j t)"), dist_b[:].rearrange("p j t -> p (j t)"), ALU.min)
+            return hid
+
+        def second_stage(h, hid):
+            hid_w = tile([P, JH], U32, "hid_w%d" % h)
+            hid_s = tile([P, JH], U8, "hid_s%d" % h)
+            nc.vector.quantize_mx(out=hid_w[:].bitcast(E4M3), scales=hid_s[:], in_=hid[:])
+            rows = []
+            for c in range(N // P):
+                cols = slice(c * P, (c + 1) * P)
+                acc = ps.tile([P, JH], F32, name="acc_p%d%d" % (h, c))
+                nc.tensor.matmul_mx(out=acc[:], lhsT=wb_w[:, cols].bitcast(E5M2), lhsT_scale=wb_s[:, cols],
+                                    rhs=hid_w[:].bitcast(E4M3), rhs_scale=hid_s[:], start=True, stop=True)
+                rows.append(acc)
+            return rows
+
+        def put(h, accs):
+            entries = page_list[:, h * (JH // 16) : (h + 1) * (JH // 16)]
+            for c in range(N // P):
+                p_sb = tile([P, JH], F32, "p_sb%d%d" % (h, c))
+                nc.vector.tensor_copy(p_sb[:], accs[c][:])
+                nc.scalar.activation(out=pages[c][:].indirect(entries), in_=p_sb[:], func=ACT.Copy, scale=so_sb[:, c : c + 1])
+                if h == HALVES - 1:
+                    nc.sync.dma_start(out[c * P : (c + 1) * P, :], pages[c][:])
+
+        da0 = distance("a", 0, acc_a[0])
+        db0 = distance("b", 0, acc_b[0])
+        da1 = distance("a", 1, acc_a[1])
+        hid0 = nearer(0, da0, db0)
+        db1 = distance("b", 1, acc_b[1])
+        p0 = second_stage(0, hid0)
+        put(0, p0)
+        hid1 = nearer(1, da1, db1)
+        p1 = second_stage(1, hid1)
+        put(1, p1)

@@ -33,8 +33,8 @@ def tile_list_nearerresult_kernel(tc, xt_words, xt_scales, xo_words, xo_scales, 
         sb = ctx.enter_context(tc.tile_pool(name="sb", bufs=1))
         ps = ctx.enter_context(tc.psum_pool(name="ps", bufs=1))
 
-        def tile(shape, dtype, name):
-            return sb.tile(shape, dtype, name=name, align_bytes=64)
+        def tile(shape, dtype, name, tag=None):
+            return sb.tile(shape, dtype, name=name, tag=tag or name, align_bytes=64)
 
         lists = [tile([P, LIST_COLS], U16, "list%d" % i) for i in range(4)]
         xt_list, xo_list, ca_list, page_list = lists
@@ -54,13 +54,13 @@ def tile_list_nearerresult_kernel(tc, xt_words, xt_scales, xo_words, xo_scales, 
         so_sb = tile([P, N // P], F32, "so_sb")
         pages = [tile([P, E], F32, "page%d" % c) for c in range(N // P)]
 
-        nc.vector.memset(xt_s[:].bitcast(I32), 0)
-        nc.vector.memset(w_s[:].rearrange("p h c -> p (h c)").bitcast(I32), 0)
-        nc.vector.memset(xo_s[:].bitcast(I32), 0)
-        nc.vector.memset(w2_s[:].rearrange("p h c -> p (h c)").bitcast(I32), 0)
-        nc.vector.memset(wb_s[:].bitcast(I32), 0)
+        for plane in (xt_s, xo_s, wb_s):
+            nc.vector.memset(plane[:].bitcast(I32), 0)
+        for plane in (w_s, w2_s):
+            nc.vector.memset(plane[:].rearrange("p h c -> p (h c)").bitcast(I32), 0)
+        nc.gpsimd.dma_start(st_sb[:], st.rearrange("(p t) o -> p (t o)", t=PACK))
         for page in pages:
-            nc.vector.memset(page[:].bitcast(I32), 0)
+            nc.gpsimd.memset(page[:], 0.0)
 
         ca_by_slot = ca.rearrange("(p t) v -> p t v", t=PACK)
 
@@ -69,32 +69,31 @@ def tile_list_nearerresult_kernel(tc, xt_words, xt_scales, xo_words, xo_scales, 
             for q in range(4):
                 queue.dma_start(plane[32 * q : 32 * q + 4, :].bitcast(I32), rows[4 * q : 4 * q + 4, :])
 
-        def load_scale_rows_paired(plane, scales):
+        def load_scale_rows_paired(queue, plane, scales):
             rows = scales[0].bitcast(I32).rearrange("(h q r) c -> q r h c", h=2, q=2)
             for q in range(2):
-                nc.sync.dma_start(plane[32 * q : 32 * q + 4, :, :].bitcast(I32), rows[q])
+                queue.dma_start(plane[32 * q : 32 * q + 4, :, :].bitcast(I32), rows[q])
 
         nc.sync.dma_start(ca_list[:], offs3)
         nc.sync.dma_start(ca_rows[0][:], ca_by_slot[:, 0, :])
-        nc.sync.dma_start(xt_list[:], offs)
-        nc.scalar.dma_start(xt_w[:].bitcast(I32), xt_words[0].rearrange("p c r -> p (c r)").bitcast(I32))
-        load_scale_rows(nc.scalar, xt_s, xt_scales)
-        nc.sync.dma_start(ca_rows[1][:], ca_by_slot[:, 1, :])
-        load_scale_rows_paired(w_s, w_scales)
-        nc.sync.dma_start(w_w[:].bitcast(I32), w_words[0].bitcast(I32))
-        nc.sync.dma_start(ca_rows[2][:], ca_by_slot[:, 2, :])
         nc.sync.dma_start(xo_list[:], offs2)
+        nc.sync.dma_start(ca_rows[1][:], ca_by_slot[:, 1, :])
         nc.sync.dma_start(xo_w[:].bitcast(I32), xo_words[0].bitcast(I32))
-        nc.sync.dma_start(w2_w[:].bitcast(I32), w2_words[0].rearrange("p c r -> p (c r)").bitcast(I32))
+        nc.sync.dma_start(ca_rows[2][:], ca_by_slot[:, 2, :])
+        nc.sync.dma_start(xt_list[:], offs)
+        nc.sync.dma_start(xt_w[:].bitcast(I32), xt_words[0].rearrange("p c r -> p (c r)").bitcast(I32))
         load_scale_rows(nc.sync, xo_s, xo_scales)
-        load_scale_rows_paired(w2_s, w2_scales)
+        load_scale_rows_paired(nc.sync, w2_s, w2_scales)
+        nc.sync.dma_start(w2_w[:].bitcast(I32), w2_words[0].rearrange("p c r -> p (c r)").bitcast(I32))
         nc.sync.dma_start(ca_rows[3][:], ca_by_slot[:, 3, :])
+        load_scale_rows(nc.sync, xt_s, xt_scales)
+        load_scale_rows_paired(nc.sync, w_s, w_scales)
+        nc.sync.dma_start(w_w[:].bitcast(I32), w_words[0].bitcast(I32))
+        nc.sync.dma_start(wb_w[:].bitcast(I32), wb_words[0].rearrange("p c r -> p (c r)").bitcast(I32))
+        load_scale_rows(nc.sync, wb_s, wb_scales)
         nc.sync.dma_start(page_list[:], offs4)
-        nc.gpsimd.dma_start(st_sb[:], st.rearrange("(p t) o -> p (t o)", t=PACK))
-        nc.gpsimd.dma_start(wb_w[:].bitcast(I32), wb_words[0].rearrange("p c r -> p (c r)").bitcast(I32))
-        load_scale_rows(nc.gpsimd, wb_s, wb_scales)
         with nc.allow_non_contiguous_dma(reason="one weight a partition for each of the two row tiles"):
-            nc.gpsimd.dma_start(so_sb[:], so.rearrange("(c p) o -> p (c o)", p=P))
+            nc.sync.dma_start(so_sb[:], so.rearrange("(c p) o -> p (c o)", p=P))
 
         ca_g = [tile([P, J], U8, "ca_g%d" % t) for t in range(PACK)]
         proto = tile([P, PACK, J], F32, "proto")
@@ -115,25 +114,28 @@ def tile_list_nearerresult_kernel(tc, xt_words, xt_scales, xo_words, xo_scales, 
             return (dst.rearrange("p (t c i) -> p c t i", t=PACK, i=run),
                     src.rearrange("p (c i t) -> p c t i", t=PACK, i=run))
 
-        def deal_scales(dst, plane):
+        def spread_scales(plane):
             nc.vector.tensor_copy(plane[64:128, 0, :].bitcast(I32), plane[0:64, 1, :].bitcast(I32))
+
+        def deal_scales(dst, plane):
+            spread_scales(plane)
             o, i = deal_views(dst[:], plane[:, 0, :], 16)
             nc.vector.tensor_copy(o, i)
 
         look_up_prototypes(0)
-        nc.vector.tensor_copy(xt_gw[:], xt_w[:].indirect(xt_list[:]))
-        nc.vector.tensor_copy(xt_gs[:], xt_s[:].indirect(xt_list[:]))
         look_up_prototypes(1)
-        o, i = deal_views(w_dw[:], w_w[:], 8)
-        nc.scalar.copy(o, i)
-        deal_scales(w_ds, w_s)
-        look_up_prototypes(2)
         nc.vector.tensor_copy(xo_gw[:], xo_w[:].indirect(xo_list[:]))
+        look_up_prototypes(2)
+        nc.vector.tensor_copy(xt_gw[:], xt_w[:].indirect(xt_list[:]))
         nc.vector.tensor_copy(xo_gs[:], xo_s[:].indirect(xo_list[:]))
+        deal_scales(w2_ds, w2_s)
         o, i = deal_views(w2_dw[:], w2_w[:], 4)
         nc.scalar.copy(o, i)
         look_up_prototypes(3)
-        deal_scales(w2_ds, w2_s)
+        nc.vector.tensor_copy(xt_gs[:], xt_s[:].indirect(xt_list[:]))
+        deal_scales(w_ds, w_s)
+        o, i = deal_views(w_dw[:], w_w[:], 8)
+        nc.scalar.copy(o, i)
 
         def first_stage(name, h, words, scales, wfmt, gwords, gscales, xfmt):
             acc = ps.tile([P, PACK, JH], F32, name="%s%d" % (name, h))
@@ -144,18 +146,18 @@ def tile_list_nearerresult_kernel(tc, xt_words, xt_scales, xo_words, xo_scales, 
                                     rhs=gwords[:, cols].bitcast(xfmt), rhs_scale=gscales[:, cols], start=True, stop=True)
             return acc
 
-        acc_a = [first_stage("acc_a", h, w_dw, w_ds, E2M1, xt_gw, xt_gs, E4M3) for h in range(HALVES)]
         acc_b = [first_stage("acc_b", h, w2_dw, w2_ds, E5M2, xo_gw, xo_gs, E2M1) for h in range(HALVES)]
+        acc_a = [first_stage("acc_a", h, w_dw, w_ds, E2M1, xt_gw, xt_gs, E4M3) for h in range(HALVES)]
 
-        def distance(name, h, acc):
-            diff = tile([P, PACK, JH], F32, "diff_%s%d" % (name, h))
+        def distance(name, h, acc, tag=None):
+            diff = tile([P, PACK, JH], F32, "diff_%s%d" % (name, h), tag)
             dist = tile([P, JH, PACK], F32, "dist_%s%d" % (name, h))
             nc.vector.tensor_tensor(diff[:], acc[:], proto[:, :, h * JH : (h + 1) * JH], ALU.subtract)
             nc.scalar.activation(out=dist[:], in_=diff[:].rearrange("p t j -> p j t"), func=ACT.Abs)
             return dist
 
         def nearer(h, dist_a, dist_b):
-            hid = tile([P, JH * PACK], BF16, "hid%d" % h)
+            hid = tile([P, JH * PACK], BF16, "hid%d" % h, "hid")
             nc.vector.tensor_tensor(hid[:], dist_a[:].rearrange("p j t -> p (j t)"), dist_b[:].rearrange("p j t -> p (j t)"), ALU.min)
             return hid
 
@@ -176,18 +178,19 @@ def tile_list_nearerresult_kernel(tc, xt_words, xt_scales, xo_words, xo_scales, 
             entries = page_list[:, h * (JH // 16) : (h + 1) * (JH // 16)]
             for c in range(N // P):
                 p_sb = tile([P, JH], F32, "p_sb%d%d" % (h, c))
-                nc.vector.tensor_copy(p_sb[:], accs[c][:])
+                if h == 0:
+                    nc.scalar.copy(p_sb[:], accs[c][:])
+                else:
+                    nc.vector.tensor_copy(p_sb[:], accs[c][:])
                 nc.scalar.activation(out=pages[c][:].indirect(entries), in_=p_sb[:], func=ACT.Copy, scale=so_sb[:, c : c + 1])
                 if h == HALVES - 1:
                     nc.sync.dma_start(out[c * P : (c + 1) * P, :], pages[c][:])
 
+        db0 = distance("b", 0, acc_b[0], "w_s")
+        db1 = distance("b", 1, acc_b[1], "w_w")
         da0 = distance("a", 0, acc_a[0])
-        db0 = distance("b", 0, acc_b[0])
         da1 = distance("a", 1, acc_a[1])
-        hid0 = nearer(0, da0, db0)
-        db1 = distance("b", 1, acc_b[1])
-        p0 = second_stage(0, hid0)
+        p0 = second_stage(0, nearer(0, da0, db0))
         put(0, p0)
-        hid1 = nearer(1, da1, db1)
-        p1 = second_stage(1, hid1)
+        p1 = second_stage(1, nearer(1, da1, db1))
         put(1, p1)

@@ -54,6 +54,11 @@ def tile_list_nearerresult_kernel(tc, xt_words, xt_scales, xo_words, xo_scales, 
         so_sb = tile([P, N // P], F32, "so_sb")
         pages = [tile([P, E], F32, "page%d" % c) for c in range(N // P)]
 
+        warm_in = tile([P, 1], F32, "warm_in")
+        warm_out = tile([P, 1], F32, "warm_out")
+        nc.vector.memset(warm_in[:], 0.0)
+        nc.scalar.activation(out=warm_out[:], in_=warm_in[:], func=ACT.Abs)
+
         for plane in (xt_s, xo_s, wb_s):
             nc.vector.memset(plane[:].bitcast(I32), 0)
         for plane in (w_s, w2_s):

@@ -87,12 +87,12 @@ def tile_list_nearerresult_kernel(tc, xt_words, xt_scales, xo_words, xo_scales, 
         nc.sync.dma_start(ca_rows[2][:], ca_by_slot[:, 2, :])
         nc.sync.dma_start(xt_list[:], offs)
         nc.sync.dma_start(xt_w[:].bitcast(I32), xt_words[0].rearrange("p c r -> p (c r)").bitcast(I32))
+        nc.sync.dma_start(w2_w[:].bitcast(I32), w2_words[0].rearrange("p c r -> p (c r)").bitcast(I32))
         load_scale_rows(nc.sync, xo_s, xo_scales)
         load_scale_rows_paired(nc.sync, w2_s, w2_scales)
-        nc.sync.dma_start(w2_w[:].bitcast(I32), w2_words[0].rearrange("p c r -> p (c r)").bitcast(I32))
         nc.sync.dma_start(ca_rows[3][:], ca_by_slot[:, 3, :])
-        load_scale_rows(nc.sync, xt_s, xt_scales)
         load_scale_rows_paired(nc.sync, w_s, w_scales)
+        load_scale_rows(nc.sync, xt_s, xt_scales)
         nc.sync.dma_start(w_w[:].bitcast(I32), w_words[0].bitcast(I32))
         nc.sync.dma_start(wb_w[:].bitcast(I32), wb_words[0].rearrange("p c r -> p (c r)").bitcast(I32))
         load_scale_rows(nc.sync, wb_s, wb_scales)
@@ -125,7 +125,7 @@ def tile_list_nearerresult_kernel(tc, xt_words, xt_scales, xo_words, xo_scales, 
         def deal_scales(dst, plane):
             spread_scales(plane)
             o, i = deal_views(dst[:], plane[:, 0, :], 16)
-            nc.vector.tensor_copy(o, i)
+            nc.gpsimd.tensor_copy(o, i)
 
         look_up_prototypes(0)
         look_up_prototypes(1)
@@ -133,12 +133,12 @@ def tile_list_nearerresult_kernel(tc, xt_words, xt_scales, xo_words, xo_scales, 
         look_up_prototypes(2)
         nc.vector.tensor_copy(xt_gw[:], xt_w[:].indirect(xt_list[:]))
         nc.vector.tensor_copy(xo_gs[:], xo_s[:].indirect(xo_list[:]))
-        deal_scales(w2_ds, w2_s)
         o, i = deal_views(w2_dw[:], w2_w[:], 4)
         nc.scalar.copy(o, i)
+        deal_scales(w2_ds, w2_s)
         look_up_prototypes(3)
-        nc.vector.tensor_copy(xt_gs[:], xt_s[:].indirect(xt_list[:]))
         deal_scales(w_ds, w_s)
+        nc.vector.tensor_copy(xt_gs[:], xt_s[:].indirect(xt_list[:]))
         o, i = deal_views(w_dw[:], w_w[:], 8)
         nc.scalar.copy(o, i)
 
@@ -154,11 +154,11 @@ def tile_list_nearerresult_kernel(tc, xt_words, xt_scales, xo_words, xo_scales, 
         acc_b = [first_stage("acc_b", h, w2_dw, w2_ds, E5M2, xo_gw, xo_gs, E2M1) for h in range(HALVES)]
         acc_a = [first_stage("acc_a", h, w_dw, w_ds, E2M1, xt_gw, xt_gs, E4M3) for h in range(HALVES)]
 
-        def distance(name, h, acc, tag=None):
-            diff = tile([P, PACK, JH], F32, "diff_%s%d" % (name, h), tag)
+        def distance(name, h, acc, diffs):
+            diff = diffs[:, h, :, :]
             dist = tile([P, JH, PACK], F32, "dist_%s%d" % (name, h))
-            nc.vector.tensor_tensor(diff[:], acc[:], proto[:, :, h * JH : (h + 1) * JH], ALU.subtract)
-            nc.scalar.activation(out=dist[:], in_=diff[:].rearrange("p t j -> p j t"), func=ACT.Abs)
+            nc.vector.tensor_tensor(diff, acc[:], proto[:, :, h * JH : (h + 1) * JH], ALU.subtract)
+            nc.scalar.activation(out=dist[:], in_=diff.rearrange("p t j -> p j t"), func=ACT.Abs)
             return dist
 
         def nearer(h, dist_a, dist_b):
@@ -183,7 +183,7 @@ def tile_list_nearerresult_kernel(tc, xt_words, xt_scales, xo_words, xo_scales, 
             entries = page_list[:, h * (JH // 16) : (h + 1) * (JH // 16)]
             for c in range(N // P):
                 p_sb = tile([P, JH], F32, "p_sb%d%d" % (h, c))
-                if h == 0:
+                if h == 0 and c == 0:
                     nc.scalar.copy(p_sb[:], accs[c][:])
                 else:
                     nc.vector.tensor_copy(p_sb[:], accs[c][:])
@@ -191,10 +191,12 @@ def tile_list_nearerresult_kernel(tc, xt_words, xt_scales, xo_words, xo_scales, 
                 if h == HALVES - 1:
                     nc.sync.dma_start(out[c * P : (c + 1) * P, :], pages[c][:])
 
-        db0 = distance("b", 0, acc_b[0], "w_s")
-        db1 = distance("b", 1, acc_b[1], "w_w")
-        da0 = distance("a", 0, acc_a[0])
-        da1 = distance("a", 1, acc_a[1])
+        diff_b = tile([P, HALVES, PACK, JH], F32, "diff_b", "xt_s")
+        diff_a = tile([P, HALVES, PACK, JH], F32, "diff_a")
+        db0 = distance("b", 0, acc_b[0], diff_b)
+        db1 = distance("b", 1, acc_b[1], diff_b)
+        da0 = distance("a", 0, acc_a[0], diff_a)
+        da1 = distance("a", 1, acc_a[1], diff_a)
         p0 = second_stage(0, nearer(0, da0, db0))
         put(0, p0)
         p1 = second_stage(1, nearer(1, da1, db1))

from contextlib import ExitStack

import concourse.mybir as mybir

K, T, J, R, N, E = 512, 1024, 256, 512, 256, 1024
FLOPS = 2 * K * R * J * 2 + 2 * R * N * J

F32 = mybir.dt.float32
BF16 = mybir.dt.bfloat16
I32 = mybir.dt.int32
U32 = mybir.dt.uint32
U16 = mybir.dt.uint16
U8 = mybir.dt.uint8
FP8 = mybir.dt.float8_e4m3fn
E4M3 = mybir.dt.float8_e4m3fn_x4
E5M2 = mybir.dt.float8_e5m2_x4
E2M1 = mybir.dt.float4_e2m1fn_x4
ACT = mybir.ActivationFunctionType
ALU = mybir.AluOpType

P = 128
PACK = 4
HALVES = 2
JH = J // HALVES
LIST_COLS = J // 16


def tile_list_nearerresult_kernel(tc, xt_words, xt_scales, xo_words, xo_scales, w_words, w_scales,
                                       w2_words, w2_scales, ca, st, wb_words, wb_scales, so,
                                       offs, offs2, offs3, offs4, out):
    nc = tc.nc
    with ExitStack() as ctx:
        sb = ctx.enter_context(tc.tile_pool(name="sb", bufs=1))
        ps = ctx.enter_context(tc.psum_pool(name="ps", bufs=1))

        def tile(shape, dtype, name, tag=None):
            return sb.tile(shape, dtype, name=name, tag=tag or name, align_bytes=64)

        lists = [tile([P, LIST_COLS], U16, "list%d" % i) for i in range(4)]
        xt_list, xo_list, ca_list, page_list = lists

        xt_w = tile([P, T], U32, "xt_w")
        xt_s = tile([P, T], U8, "xt_s")
        xo_w = tile([P, T], U16, "xo_w")
        xo_s = tile([P, T], U8, "xo_s")
        w_w = tile([P, R], U16, "w_w")
        w_s = tile([P, 2, R], U8, "w_s")
        w2_w = tile([P, R], U32, "w2_w")
        w2_s = tile([P, 2, R], U8, "w2_s")
        wb_w = tile([P, N], U32, "wb_w")
        wb_s = tile([P, N], U8, "wb_s")
        ca_rows = [tile([P, T], U8, "ca_rows%d" % t) for t in range(PACK)]
        st_sb = tile([P, PACK], F32, "st_sb")
        so_sb = tile([P, N // P], F32, "so_sb")
        pages = [tile([P, E], F32, "page%d" % c) for c in range(N // P)]

        warm_in = tile([P, 1], F32, "warm_in")
        warm_out = tile([P, 1], F32, "warm_out")
        nc.vector.memset(warm_in[:], 0.0)
        nc.scalar.activation(out=warm_out[:], in_=warm_in[:], func=ACT.Abs)

        for plane in (xt_s, xo_s, wb_s):
            nc.vector.memset(plane[:].bitcast(I32), 0)
        for plane in (w_s, w2_s):
            nc.vector.memset(plane[:].rearrange("p h c -> p (h c)").bitcast(I32), 0)
        nc.gpsimd.dma_start(st_sb[:], st.rearrange("(p t) o -> p (t o)", t=PACK))
        for page in pages:
            nc.gpsimd.memset(page[:], 0.0)

        ca_by_slot = ca.rearrange("(p t) v -> p t v", t=PACK)

        def load_scale_rows(queue, plane, scales):
            rows = scales[0].bitcast(I32)
            for q in range(4):
                queue.dma_start(plane[32 * q : 32 * q + 4, :].bitcast(I32), rows[4 * q : 4 * q + 4, :])

        def load_scale_rows_paired(queue, plane, scales):
            rows = scales[0].bitcast(I32).rearrange("(h q r) c -> q r h c", h=2, q=2)
            for q in range(2):
                queue.dma_start(plane[32 * q : 32 * q + 4, :, :].bitcast(I32), rows[q])

        nc.sync.dma_start(ca_list[:], offs3)
        nc.sync.dma_start(ca_rows[0][:], ca_by_slot[:, 0, :])
        nc.sync.dma_start(xo_list[:], offs2)
        nc.sync.dma_start(ca_rows[1][:], ca_by_slot[:, 1, :])
        nc.sync.dma_start(xo_w[:].bitcast(I32), xo_words[0].bitcast(I32))
        nc.sync.dma_start(ca_rows[2][:], ca_by_slot[:, 2, :])
        nc.sync.dma_start(xt_list[:], offs)
        nc.sync.dma_start(xt_w[:].bitcast(I32), xt_words[0].rearrange("p c r -> p (c r)").bitcast(I32))
        nc.sync.dma_start(w2_w[:].bitcast(I32), w2_words[0].rearrange("p c r -> p (c r)").bitcast(I32))
        load_scale_rows(nc.sync, xo_s, xo_scales)
        load_scale_rows_paired(nc.sync, w2_s, w2_scales)
        nc.sync.dma_start(ca_rows[3][:], ca_by_slot[:, 3, :])
        load_scale_rows_paired(nc.sync, w_s, w_scales)
        load_scale_rows(nc.sync, xt_s, xt_scales)
        nc.sync.dma_start(w_w[:].bitcast(I32), w_words[0].bitcast(I32))
        nc.sync.dma_start(wb_w[:].bitcast(I32), wb_words[0].rearrange("p c r -> p (c r)").bitcast(I32))
        load_scale_rows(nc.sync, wb_s, wb_scales)
        nc.sync.dma_start(page_list[:], offs4)
        with nc.allow_non_contiguous_dma(reason="one weight a partition for each of the two row tiles"):
            nc.sync.dma_start(so_sb[:], so.rearrange("(c p) o -> p (c o)", p=P))

        ca_g = [tile([P, J], U8, "ca_g%d" % t) for t in range(PACK)]
        proto = tile([P, PACK, J], F32, "proto")
        xt_gw = tile([P, J], U32, "xt_gw")
        xt_gs = tile([P, J], U8, "xt_gs")
        xo_gw = tile([P, J], U16, "xo_gw")
        xo_gs = tile([P, J], U8, "xo_gs")
        w_dw = tile([P, R], U16, "w_dw")
        w_ds = tile([P, R], U8, "w_ds")
        w2_dw = tile([P, R], U32, "w2_dw")
        w2_ds = tile([P, R], U8, "w2_ds")

        def look_up_prototypes(t):
            nc.vector.tensor_copy(ca_g[t][:], ca_rows[t][:].indirect(ca_list[:]))
            nc.scalar.activation(out=proto[:, t, :], in_=ca_g[t][:].bitcast(FP8), func=ACT.Copy, scale=st_sb[:, t : t + 1])

        def deal_views(dst, src, run):
            return (dst.rearrange("p (t c i) -> p c t i", t=PACK, i=run),
                    src.rearrange("p (c i t) -> p c t i", t=PACK, i=run))

        def spread_scales(plane):
            nc.vector.tensor_copy(plane[64:128, 0, :].bitcast(I32), plane[0:64, 1, :].bitcast(I32))

        def deal_scales(dst, plane):
            spread_scales(plane)
            o, i = deal_views(dst[:], plane[:, 0, :], 16)
            nc.gpsimd.tensor_copy(o, i)

        look_up_prototypes(0)
        look_up_prototypes(1)
        nc.vector.tensor_copy(xo_gw[:], xo_w[:].indirect(xo_list[:]))
        look_up_prototypes(2)
        nc.vector.tensor_copy(xt_gw[:], xt_w[:].indirect(xt_list[:]))
        nc.vector.tensor_copy(xo_gs[:], xo_s[:].indirect(xo_list[:]))
        o, i = deal_views(w2_dw[:], w2_w[:], 4)
        nc.scalar.copy(o, i)
        deal_scales(w2_ds, w2_s)
        look_up_prototypes(3)
        deal_scales(w_ds, w_s)
        nc.vector.tensor_copy(xt_gs[:], xt_s[:].indirect(xt_list[:]))
        o, i = deal_views(w_dw[:], w_w[:], 8)
        nc.scalar.copy(o, i)

        def first_stage(name, h, words, scales, wfmt, gwords, gscales, xfmt):
            acc = ps.tile([P, PACK, JH], F32, name="%s%d" % (name, h))
            cols = slice(h * JH, (h + 1) * JH)
            for t in range(PACK):
                rows = slice(t * P, (t + 1) * P)
                nc.tensor.matmul_mx(out=acc[:, t, :], lhsT=words[:, rows].bitcast(wfmt), lhsT_scale=scales[:, rows],
                                    rhs=gwords[:, cols].bitcast(xfmt), rhs_scale=gscales[:, cols], start=True, stop=True)
            return acc

        acc_b = [first_stage("acc_b", h, w2_dw, w2_ds, E5M2, xo_gw, xo_gs, E2M1) for h in range(HALVES)]
        acc_a = [first_stage("acc_a", h, w_dw, w_ds, E2M1, xt_gw, xt_gs, E4M3) for h in range(HALVES)]

        def distance(name, h, acc, diffs):
            diff = diffs[:, h, :, :]
            dist = tile([P, JH, PACK], F32, "dist_%s%d" % (name, h))
            nc.vector.tensor_tensor(diff, acc[:], proto[:, :, h * JH : (h + 1) * JH], ALU.subtract)
            nc.scalar.activation(out=dist[:], in_=diff.rearrange("p t j -> p j t"), func=ACT.Abs)
            return dist

        def nearer(h, dist_a, dist_b):
            hid = tile([P, JH * PACK], BF16, "hid%d" % h, "hid")
            nc.vector.tensor_tensor(hid[:], dist_a[:].rearrange("p j t -> p (j t)"), dist_b[:].rearrange("p j t -> p (j t)"), ALU.min)
            return hid

        def second_stage(h, hid):
            hid_w = tile([P, JH], U32, "hid_w%d" % h)
            hid_s = tile([P, JH], U8, "hid_s%d" % h)
            nc.vector.quantize_mx(out=hid_w[:].bitcast(E4M3), scales=hid_s[:], in_=hid[:])
            rows = []
            for c in range(N // P):
                cols = slice(c * P, (c + 1) * P)
                acc = ps.tile([P, JH], F32, name="acc_p%d%d" % (h, c))
                nc.tensor.matmul_mx(out=acc[:], lhsT=wb_w[:, cols].bitcast(E5M2), lhsT_scale=wb_s[:, cols],
                                    rhs=hid_w[:].bitcast(E4M3), rhs_scale=hid_s[:], start=True, stop=True)
                rows.append(acc)
            return rows

        def put(h, accs):
            entries = page_list[:, h * (JH // 16) : (h + 1) * (JH // 16)]
            for c in range(N // P):
                p_sb = tile([P, JH], F32, "p_sb%d%d" % (h, c))
                if h == 0 and c == 0:
                    nc.scalar.copy(p_sb[:], accs[c][:])
                else:
                    nc.vector.tensor_copy(p_sb[:], accs[c][:])
                nc.scalar.activation(out=pages[c][:].indirect(entries), in_=p_sb[:], func=ACT.Copy, scale=so_sb[:, c : c + 1])
                if h == HALVES - 1:
                    nc.sync.dma_start(out[c * P : (c + 1) * P, :], pages[c][:])

        diff_b = tile([P, HALVES, PACK, JH], F32, "diff_b", "xt_s")
        diff_a = tile([P, HALVES, PACK, JH], F32, "diff_a")
        db0 = distance("b", 0, acc_b[0], diff_b)
        db1 = distance("b", 1, acc_b[1], diff_b)
        da0 = distance("a", 0, acc_a[0], diff_a)
        da1 = distance("a", 1, acc_a[1], diff_a)
        p0 = second_stage(0, nearer(0, da0, db0))
        put(0, p0)
        p1 = second_stage(1, nearer(1, da1, db1))
        put(1, p1)
